import numpy as np, ml_dtypes
CORES = [78,86,94,102,110,118]
N = 6
J, Q = 256, 4096
def entries(a): return a.T.reshape(-1)
def pack(v, P): return np.ascontiguousarray(np.asarray(v, np.int32).reshape(-1, P).T)
def split(rng, total, parts):
    c = np.sort(rng.integers(0, total + 1, parts - 1)); return np.diff(np.concatenate([[0], c, [total]]))
def lists(rng, how):
    s = np.concatenate([[0], rng.integers(1 - Q // 2, Q // 2 + 1, N - 1), [int(rng.integers(1 - Q // 2, 1))]])
    if how == "early": s[1:] = -Q; s[N] = -2 * Q
    if how == "late": s[1:] = Q; s[N] = 0
    if how == "long":
        z = int(rng.integers(1, N - 1)); s[1:z] = -rng.integers(1, Q, z - 1); s[z] = -Q; s[z + 1] = Q; s[z + 2:N] = rng.integers(1, Q, N - z - 2); s[N] = -int(rng.integers(0, Q - s[N - 1] + 1))
    if how == "sway":
        z = int(rng.integers(1, N - 2)); e = int(rng.integers(z + 1, N - 1)); s[1:] = -rng.integers(Q // 2 + 1, Q, N); s[z + 1:e + 1] = rng.integers(Q // 2 + 1, Q - 1, e - z); s[e + 1] = s[e] - Q; s[N] = s[N - 1] - Q + int(rng.integers(1, -s[N - 1]))
    tot = Q + np.diff(s)
    L = np.stack([split(rng, int(t), J) for t in tot])
    if how == "gaps":
        L = np.zeros((N, J), np.int64)
        for r in range(N): m = 1 if r & 1 else 8; L[r, 1 + rng.permutation(J - 2)[:m]] = split(rng, int(tot[r]), m)
    if how == "long":
        L = np.zeros((N, J), np.int64); L[np.arange(N), rng.integers(0, J, N)] = tot
    return {"ln": np.stack([pack(l, 16) for l in L])}
def setup_inputs(rng):
    return dict({"x": rng.standard_normal((N, 128, J), dtype=np.float32).astype(ml_dtypes.bfloat16)}, **lists(rng, "uniform"))
def setup_inputs_early(rng):
    d = setup_inputs(rng); d.update(lists(rng, "early"))
    for k in ("x",): d[k] = (d[k].astype(np.float32) * 1048576.0).astype(d[k].dtype)
    return d
def setup_inputs_gaps(rng):
    d = setup_inputs(rng); d.update(lists(rng, "gaps"))
    for k in ("x",): d[k] = (d[k].astype(np.float32) * (1 / 1024.0)).astype(d[k].dtype)
    return d
def setup_inputs_late(rng):
    d = setup_inputs(rng); d.update(lists(rng, "late"))
    return d
def setup_inputs_long(rng):
    d = setup_inputs(rng); d.update(lists(rng, "long"))
    return d
def setup_inputs_sway(rng):
    d = setup_inputs(rng); d.update(lists(rng, "sway"))
    return d
def check_inputs(x):
    bad = []
    if x["ln"].min() < 0 or x["ln"].max() >= N * Q + 1: bad.append("ln out of range")
    if int(x["ln"].sum()) > N * Q: bad.append("the lengths come to more than N * Q")
    c = np.concatenate([[0], np.cumsum([int(a.sum()) for a in x["ln"]])])
    if any(c[r] < (r - 1) * Q or c[r + 1] > (r + 2) * Q for r in range(N)): bad.append("the sums of the lengths before or up to a rank leave their bounds")
    return bad
def reference(x, ln):
    got = np.concatenate([np.repeat(x[r], entries(ln[r]), axis=1) for r in range(N)], axis=1)[:, :N * Q]
    Y = np.zeros((128, N * Q), x.dtype); Y[:, :got.shape[1]] = got
    return {"y": np.stack([Y[:, Q * r:Q * r + Q] for r in range(N)])}

@@ -1,0 +1,224 @@
+from concourse.bass import DstId, RemoteDMATransfer
+from concourse.mybir import AluOpType, ActivationFunctionType
+
+N, J, Q = 6, 256, 4096
+MAGIC = 201326592.0
+
+SCRATCH = {
+    "lnd": ("dram", [N * 128, 2], "int32"),
+    "lni": ("sbuf", [128, 16 * N], "int32"),
+    "lnf": ("sbuf", [128, 16 * N], "float32"),
+    "pref": ("sbuf", [128, 16 * N + 4], "float32"),
+    "ones": ("sbuf", [128, 128], "float32"),
+    "tri": ("sbuf", [128, 128], "float32"),
+    "qi": ("sbuf", [128, 1], "int32"),
+    "qa": ("sbuf", [128, 1], "int32"),
+    "qb": ("sbuf", [128, 1], "int32"),
+    "qc": ("sbuf", [128, 1], "int32"),
+    "qd": ("sbuf", [128, 1], "int32"),
+    "off6": ("sbuf", [128, 2], "uint16"),
+    "eh": ("sbuf", [128, 96], "float32"),
+    "e6": ("sbuf", [128, 16], "float32"),
+    "iop": ("sbuf", [128, 128], "bfloat16"),
+    "i16": ("sbuf", [128, 264], "bfloat16"),
+    "ios": ("sbuf", [128, 264], "float32"),
+    "la": ("sbuf", [128, 6 * 128], "bfloat16"),
+    "lb": ("sbuf", [128, 6 * 128], "bfloat16"),
+    "rr": ("sbuf", [128, 6 * 264], "bfloat16"),
+    "off": ("sbuf", [128, 256], "uint16"),
+    "win": ("sbuf", [128, 776], "bfloat16"),
+    "yt": ("sbuf", [128, Q], "bfloat16"),
+    "pe": ("psum", [128, 512], "float32"),
+    "p0": ("psum", [128, 512], "float32"),
+    "p1": ("psum", [128, 512], "float32"),
+    "p2": ("psum", [128, 512], "float32"),
+    "p3": ("psum", [128, 512], "float32"),
+}
+SEMAPHORES = (["ldl", "ldx", "lnin", "lnarr", "xarr", "lsl", "lsx", "one", "tri", "qi", "qs", "i16", "ios", "set", "conv",
+               "scan", "e48", "eh", "e6", "st"]
+              + ["ch%d" % t for t in range(6)] + ["pq%d" % q for q in range(4)] + ["of%d" % q for q in range(4)]
+              + ["gv%d" % k for k in range(5)] + ["gs%d" % k for k in range(5)])
+
+
+def bits_of(m):
+    return [b for b in range(16) if m >> b & 1]
+
+
+def rank_program(g, core, T, topo):
+    r = T.rank_of(core)
+    if r is None:
+        return
+    S = T.sem
+    A = AluOpType
+    F = ActivationFunctionType
+    v, s, pe, sy = g.vector, g.scalar, g.tensor, g.sync
+    near = [i for i in (r - 1, r, r + 1) if 0 <= i < N]
+    nn = len(near)
+    nc = 2 * nn
+    nf = near[0]
+    ncol = 16 * (near[-1] + 1)
+    c0 = 16 * near[0]
+    w16 = 16 * nn
+    lo = 256 * (near[0] - (r - 1))
+    tail = 1 if r >= N - 2 else 0
+    whi = lo + 256 * nn + tail
+    s_chunks = [0, 2, 3, 5] if nc == 6 else [0, 2]
+
+    def dest(i):
+        rid, pid, _ = topo.addr(T.cores[i])
+        return DstId(rid=rid, pnc=pid)
+
+    def two_hops_first(ranks):
+        return sorted(ranks, key=lambda i: topo.mates(topo.chip(core), topo.chip(T.cores[i])))
+
+    sy.dma_start(T.lnd[128 * r:128 * r + 128, :], T.ln[:]).then_inc(S.ldl, 16)
+    s.dma_start(T.win[:, 256:512], T.x[:]).then_inc(S.ldx, 16)
+    s.dma_start(T.lni[0:16, 16 * r:16 * r + 16], T.ln[:]).then_inc(S.lnin, 16)
+
+    g.iota(T.qi[:], [[0, 1]], 0, 1).then_inc(S.qi, 1)
+    g.wait_ge(S.one, 1)
+    g.affine_select(T.tri[0:16, :], T.ones[0:16, :], [[0, 8], [1, 16]], A.is_ge, 0.0, 0, -1).then_inc(S.tri, 1)
+
+    ln_to = two_hops_first([i for i in range(N) if i > r or i == r - 1])
+    x_to = two_hops_first([i for i in (r - 1, r + 1) if 0 <= i < N])
+    full = topo.mask(core, T.cores[ln_to[0]])
+    for i in ln_to:
+        full &= topo.mask(core, T.cores[i])
+    ebits = bits_of(full)
+    few = [b for b in ebits if b % 4 == 0]
+    nfew = len(few)
+    nful = len(ebits)
+    fmask = sum(1 << b for b in few)
+    g.wait_ge(S.ldl, 16)
+    src = T.lnd[128 * r:128 * r + 128, :]
+    g.remote_dma_fused([RemoteDMATransfer(dst_ids=[dest(i) for i in ln_to], dma_engine_mask=fmask, remote_sem=S.lnarr,
+                                          srcs=[src], dsts=[src for i in ln_to])], local_sem=S.lsl)
+    g.wait_ge(S.ldx, 16)
+    g.remote_dma_fused([RemoteDMATransfer(dst_ids=[dest(i) for i in x_to], dma_engine_mask=full, remote_sem=S.xarr,
+                                          srcs=[T.win[:, 256:512]],
+                                          dsts=[T.win[:, 256 * (r - i + 1):256 * (r - i + 1) + 256] for i in x_to])],
+                       local_sem=S.lsx)
+    g.iota(T.i16[:, 0:257], [[16, 257]], -16, 0, allow_small_or_imprecise_dtypes=True).then_inc(S.i16, 1)
+    g.wait_ge(S.lsl, nfew)
+    g.wait_ge(S.lsx, nful)
+
+    ln_from = [i for i in range(N) if i != r and (i < r or i == r + 1)]
+    x_from = [i for i in near if i != r]
+    nld = 1
+
+    def load_list(queue, i):
+        queue.dma_start(T.lni[0:16, 16 * i:16 * i + 16], T.lnd[128 * i:128 * i + 128, :]).then_inc(S.lnin, 16)
+
+    sy.wait_ge(S.lnarr, nfew * len(ln_from))
+    if nf:
+        sy.dma_start(T.lni[0:16, 0:16 * nf], T.lnd[0:128 * nf, :]).then_inc(S.lnin, 16)
+        nld += 1
+    if r + 1 < N:
+        load_list(sy, r + 1)
+        nld += 1
+    if r > 0:
+        s.wait_ge(S.lnarr, nfew * len(ln_from))
+        load_list(s, r - 1)
+        nld += 1
+
+    start = (-float(Q) * r - 7.5) / 16.0
+    v.memset(T.ones[0:16, :], 1.0).then_inc(S.one, 1)
+    nset = 1
+    v.memset(T.pref[0:16, 0:1], start).then_inc(S.set, 1)
+    for p in range(16):
+        v.memset(T.iop[:, p:128:16], p - 7.5).then_inc(S.set, 1)
+        nset += 1
+    if tail:
+        v.memset(T.win[:, lo + 256 * nn:lo + 256 * nn + 8], 0.0).then_inc(S.set, 1)
+        nset += 1
+    v.wait_ge(S.qi, 1)
+    v.tensor_scalar(T.qa[:], T.qi[:], 15, None, A.bitwise_and).then_inc(S.qs, 1)
+    v.tensor_scalar(T.qb[:], T.qi[:], 4, None, A.logical_shift_right).then_inc(S.qs, 1)
+    v.wait_ge(S.qs, 2)
+    v.tensor_scalar(T.qc[:], T.qa[:], 8.0, None, A.mult).then_inc(S.qs, 1)
+    v.wait_ge(S.qs, 3)
+    v.tensor_tensor(T.qd[:], T.qc[:], T.qb[:], A.add).then_inc(S.qs, 1)
+    v.wait_ge(S.qs, 4)
+    v.tensor_scalar(T.off6[:, 0:1], T.qd[:], float(2 * w16 - 1), None, A.min).then_inc(S.qs, 1)
+    v.wait_ge(S.i16, 1)
+    v.tensor_scalar(T.ios[:, 0:257], T.i16[:, 0:257], -1.0, -8.0, A.mult, A.add).then_inc(S.ios, 1)
+
+    v.wait_ge(S.lnin, 16 * nld)
+    v.tensor_copy(T.lnf[0:16, 0:ncol], T.lni[0:16, 0:ncol]).then_inc(S.conv, 1)
+    v.wait_ge(S.one, 1)
+    v.wait_ge(S.conv, 1)
+    v.tensor_tensor_scan(T.pref[0:16, 1:ncol + 1], T.ones[0:16, 0:ncol], T.lnf[0:16, 0:ncol], start,
+                         A.mult, A.add).then_inc(S.scan, 1)
+    pe.wait_ge(S.tri, 1)
+    pe.wait_ge(S.one, 1)
+    pe.wait_ge(S.set, nset)
+    pe.wait_ge(S.conv, 1)
+    pe.matmul(T.pe[:, 0:w16], T.tri[0:16, :], T.lnf[0:16, c0:c0 + w16], True, False)
+    pe.wait_ge(S.scan, 1)
+    pe.matmul(T.pe[:, 0:w16], T.ones[0:16, :], T.pref[0:16, c0:c0 + w16], False, True).then_inc(S.e48, 1)
+    v.wait_ge(S.e48, 1)
+    v.tensor_copy(T.eh[:, 0:w16], T.pe[:, 0:w16]).then_inc(S.eh, 1)
+    v.tensor_scalar(T.eh[:, w16:2 * w16], T.pe[:, 0:w16], MAGIC, MAGIC, A.add, A.subtract).then_inc(S.eh, 1)
+    v.wait_ge(S.qs, 5)
+    v.wait_ge(S.eh, 2)
+    v.tensor_copy(T.e6[:], T.eh[:, 0:2 * w16].indirect(T.off6[:, 0:1])).then_inc(S.e6, 1)
+
+    v.wait_ge(S.set, nset)
+    v.wait_ge(S.e6, 1)
+    s.wait_ge(S.ios, 1)
+    s.wait_ge(S.e6, 1)
+    for t in range(nc):
+        ch = S["ch%d" % t]
+        e = T.e6[:, t:t + 1]
+        h = T.e6[:, nc + t:nc + t + 1]
+        R = T.rr[:, 264 * t:264 * t + 257]
+        v.tensor_scalar(T.la[:, 128 * t:128 * t + 128], T.iop[:], h, e, A.add, A.is_ge).then_inc(ch, 1)
+        v.tensor_scalar(T.lb[:, 128 * t:128 * t + 128], T.iop[:], h, e, A.add, A.is_lt).then_inc(ch, 1)
+        if t in s_chunks:
+            s.activation(R, T.ios[:, 0:257], F.Sign, bias=h, scale=1.0).then_inc(ch, 1)
+        else:
+            v.tensor_scalar(R, T.i16[:, 0:257], h, -2.0, A.is_ge, A.mult).then_inc(ch, 1)
+
+    order = [(0, t) for t in range(nc)]
+    order.insert(3, (1, 0))
+    order += [(1, t) for t in range(1, nc)] + [(q, t) for q in (2, 3) for t in range(nc)]
+    seen = []
+    for q, t in order:
+        if t not in seen:
+            pe.wait_ge(S["ch%d" % t], 3)
+            seen.append(t)
+        out = T["p%d" % q][:, 0:64]
+        b = 264 * t + 64 * q
+        pe.matmul(out, T.la[:, 128 * t:128 * t + 128], T.rr[:, b + 1:b + 65], t == 0, False)
+        m = pe.matmul(out, T.lb[:, 128 * t:128 * t + 128], T.rr[:, b:b + 64], False, t == nc - 1)
+        if t == nc - 1:
+            m.then_inc(S["pq%d" % q], 1)
+
+    W = T.win[:, lo:whi]
+    v_pieces = [[(0, 32)], [(64, 96)], [(128, 160)], [(192, 208), (224, 240)]]
+    s_pieces = [[(32, 64)], [(96, 128)], [(160, 192)], [(208, 224), (240, 256)]]
+    kv, ks = 0, 0
+    sts = 0
+    s.wait_ge(S.set, nset)
+    for q in range(4):
+        of = S["of%d" % q]
+        v.wait_ge(S["pq%d" % q], 1)
+        v.tensor_scalar(T.off[:, 64 * q:64 * q + 64], T["p%d" % q][:, 0:64], -128.0 * len(s_chunks), -0.5,
+                        A.add, A.mult).then_inc(of, 1)
+        v.wait_ge(of, 1)
+        s.wait_ge(of, 1)
+        if q == 0:
+            for eng in (v, s):
+                eng.wait_ge(S.ldx, 16)
+                eng.wait_ge(S.xarr, nful * len(x_from))
+        for (va, vb), (sa, sb) in zip(v_pieces[q], s_pieces[q]):
+            v.tensor_copy(T.yt[:, 16 * va:16 * vb], W.indirect(T.off[:, va:vb])).then_inc(S["gv%d" % kv], 1)
+            s.activation(T.yt[:, 16 * sa:16 * sb], W.indirect(T.off[:, sa:sb]), F.Copy).then_inc(S["gs%d" % ks], 1)
+            sy.wait_ge(S["gv%d" % kv], 1)
+            sy.dma_start(T.y[:, 16 * va:16 * vb], T.yt[:, 16 * va:16 * vb]).then_inc(S.st, 16)
+            sy.wait_ge(S["gs%d" % ks], 1)
+            sy.dma_start(T.y[:, 16 * sa:16 * sb], T.yt[:, 16 * sa:16 * sb]).then_inc(S.st, 16)
+            kv += 1
+            ks += 1
+            sts += 2
+    sy.wait_ge(S.st, 16 * sts)

@@ -36,8 +36,8 @@ SCRATCH = {
 }
 SEMAPHORES = (["ldl", "ldx", "lnin", "lnarr", "xarr", "lsl", "lsx", "one", "tri", "qi", "qs", "i16", "ios", "set", "conv",
                "scan", "e48", "eh", "e6", "st"]
-              + ["ch%d" % t for t in range(6)] + ["pq%d" % q for q in range(4)] + ["of%d" % q for q in range(4)]
-              + ["gv%d" % k for k in range(5)] + ["gs%d" % k for k in range(5)])
+              + ["ch%d" % t for t in range(6)] + ["rb%d" % t for t in range(6)] + ["pq%d" % q for q in range(4)]
+              + ["of%d" % q for q in range(4)] + ["gy%d" % k for k in range(6)])
 
 
 def bits_of(m):
@@ -62,14 +62,15 @@ def rank_program(g, core, T, topo):
     lo = 256 * (near[0] - (r - 1))
     tail = 1 if r >= N - 2 else 0
     whi = lo + 256 * nn + tail
-    s_chunks = [0, 2, 3, 5] if nc == 6 else [0, 2]
+    s_chunks = [t for t in range(nc) if t % 2 == 1]
+    v_chunks = [t for t in range(nc) if t % 2 == 0]
 
     def dest(i):
         rid, pid, _ = topo.addr(T.cores[i])
         return DstId(rid=rid, pnc=pid)
 
-    def two_hops_first(ranks):
-        return sorted(ranks, key=lambda i: topo.mates(topo.chip(core), topo.chip(T.cores[i])))
+    def is_mate(i):
+        return topo.mates(topo.chip(core), topo.chip(T.cores[i]))
 
     sy.dma_start(T.lnd[128 * r:128 * r + 128, :], T.ln[:]).then_inc(S.ldl, 16)
     s.dma_start(T.win[:, 256:512], T.x[:]).then_inc(S.ldx, 16)
@@ -79,8 +80,8 @@ def rank_program(g, core, T, topo):
     g.wait_ge(S.one, 1)
     g.affine_select(T.tri[0:16, :], T.ones[0:16, :], [[0, 8], [1, 16]], A.is_ge, 0.0, 0, -1).then_inc(S.tri, 1)
 
-    ln_to = two_hops_first([i for i in range(N) if i > r or i == r - 1])
-    x_to = two_hops_first([i for i in (r - 1, r + 1) if 0 <= i < N])
+    ln_to = sorted([i for i in range(N) if i > r or i == r - 1], key=lambda i: (i in (0, N - 1), is_mate(i)))
+    x_to = sorted([i for i in near if i != r], key=is_mate)
     full = topo.mask(core, T.cores[ln_to[0]])
     for i in ln_to:
         full &= topo.mask(core, T.cores[i])
@@ -98,7 +99,6 @@ def rank_program(g, core, T, topo):
                                           srcs=[T.win[:, 256:512]],
                                           dsts=[T.win[:, 256 * (r - i + 1):256 * (r - i + 1) + 256] for i in x_to])],
                        local_sem=S.lsx)
-    g.iota(T.i16[:, 0:257], [[16, 257]], -16, 0, allow_small_or_imprecise_dtypes=True).then_inc(S.i16, 1)
     g.wait_ge(S.lsl, nfew)
     g.wait_ge(S.lsx, nful)
 
@@ -125,6 +125,7 @@ def rank_program(g, core, T, topo):
     v.memset(T.ones[0:16, :], 1.0).then_inc(S.one, 1)
     nset = 1
     v.memset(T.pref[0:16, 0:1], start).then_inc(S.set, 1)
+    v.memset(T.i16[:, 0:1], -16.0).then_inc(S.i16, 1)
     for p in range(16):
         v.memset(T.iop[:, p:128:16], p - 7.5).then_inc(S.set, 1)
         nset += 1
@@ -140,7 +141,14 @@ def rank_program(g, core, T, topo):
     v.tensor_tensor(T.qd[:], T.qc[:], T.qb[:], A.add).then_inc(S.qs, 1)
     v.wait_ge(S.qs, 4)
     v.tensor_scalar(T.off6[:, 0:1], T.qd[:], float(2 * w16 - 1), None, A.min).then_inc(S.qs, 1)
-    v.wait_ge(S.i16, 1)
+    have, ni = 1, 1
+    while have < 257:
+        n = min(have, 257 - have)
+        v.wait_ge(S.i16, ni)
+        v.tensor_scalar(T.i16[:, have:have + n], T.i16[:, 0:n], 16.0 * have, None, A.add).then_inc(S.i16, 1)
+        have += n
+        ni += 1
+    v.wait_ge(S.i16, ni)
     v.tensor_scalar(T.ios[:, 0:257], T.i16[:, 0:257], -1.0, -8.0, A.mult, A.add).then_inc(S.ios, 1)
 
     v.wait_ge(S.lnin, 16 * nld)
@@ -163,6 +171,12 @@ def rank_program(g, core, T, topo):
     v.wait_ge(S.eh, 2)
     v.tensor_copy(T.e6[:], T.eh[:, 0:2 * w16].indirect(T.off6[:, 0:1])).then_inc(S.e6, 1)
 
+    HALF = 129
+
+    def v_right(t, a, b, sem):
+        v.tensor_scalar(T.rr[:, 264 * t + a:264 * t + b], T.i16[:, a:b], T.e6[:, nc + t:nc + t + 1], -2.0,
+                        A.is_ge, A.mult).then_inc(sem, 1)
+
     v.wait_ge(S.set, nset)
     v.wait_ge(S.e6, 1)
     s.wait_ge(S.ios, 1)
@@ -171,54 +185,73 @@ def rank_program(g, core, T, topo):
         ch = S["ch%d" % t]
         e = T.e6[:, t:t + 1]
         h = T.e6[:, nc + t:nc + t + 1]
-        R = T.rr[:, 264 * t:264 * t + 257]
         v.tensor_scalar(T.la[:, 128 * t:128 * t + 128], T.iop[:], h, e, A.add, A.is_ge).then_inc(ch, 1)
         v.tensor_scalar(T.lb[:, 128 * t:128 * t + 128], T.iop[:], h, e, A.add, A.is_lt).then_inc(ch, 1)
         if t in s_chunks:
-            s.activation(R, T.ios[:, 0:257], F.Sign, bias=h, scale=1.0).then_inc(ch, 1)
+            s.activation(T.rr[:, 264 * t:264 * t + 257], T.ios[:, 0:257], F.Sign, bias=h, scale=1.0).then_inc(ch, 1)
         else:
-            v.tensor_scalar(R, T.i16[:, 0:257], h, -2.0, A.is_ge, A.mult).then_inc(ch, 1)
+            v_right(t, 0, HALF, ch)
 
-    order = [(0, t) for t in range(nc)]
-    order.insert(3, (1, 0))
-    order += [(1, t) for t in range(1, nc)] + [(q, t) for q in (2, 3) for t in range(nc)]
-    seen = []
-    for q, t in order:
-        if t not in seen:
-            pe.wait_ge(S["ch%d" % t], 3)
-            seen.append(t)
-        out = T["p%d" % q][:, 0:64]
-        b = 264 * t + 64 * q
-        pe.matmul(out, T.la[:, 128 * t:128 * t + 128], T.rr[:, b + 1:b + 65], t == 0, False)
-        m = pe.matmul(out, T.lb[:, 128 * t:128 * t + 128], T.rr[:, b:b + 64], False, t == nc - 1)
-        if t == nc - 1:
-            m.then_inc(S["pq%d" % q], 1)
+    for q in range(4):
+        for t in range(nc):
+            if q == 0:
+                pe.wait_ge(S["ch%d" % t], 3)
+            if q == 2 and t in v_chunks:
+                pe.wait_ge(S["rb%d" % t], 1)
+            out = T["p%d" % q][:, 0:64]
+            b = 264 * t + 64 * q
+            pe.matmul(out, T.la[:, 128 * t:128 * t + 128], T.rr[:, b + 1:b + 65], t == 0, False)
+            m = pe.matmul(out, T.lb[:, 128 * t:128 * t + 128], T.rr[:, b:b + 64], False, t == nc - 1)
+            if t == nc - 1:
+                m.then_inc(S["pq%d" % q], 1)
 
     W = T.win[:, lo:whi]
-    v_pieces = [[(0, 32)], [(64, 96)], [(128, 160)], [(192, 208), (224, 240)]]
-    s_pieces = [[(32, 64)], [(96, 128)], [(160, 192)], [(208, 224), (240, 256)]]
-    kv, ks = 0, 0
-    sts = 0
-    s.wait_ge(S.set, nset)
-    for q in range(4):
-        of = S["of%d" % q]
+
+    def counts_to_offsets(q):
         v.wait_ge(S["pq%d" % q], 1)
         v.tensor_scalar(T.off[:, 64 * q:64 * q + 64], T["p%d" % q][:, 0:64], -128.0 * len(s_chunks), -0.5,
-                        A.add, A.mult).then_inc(of, 1)
-        v.wait_ge(of, 1)
-        s.wait_ge(of, 1)
+                        A.add, A.mult).then_inc(S["of%d" % q], 1)
+
+    def v_gather(k, a, b):
+        v.tensor_copy(T.yt[:, 16 * a:16 * b], W.indirect(T.off[:, a:b])).then_inc(S["gy%d" % k], 1)
+
+    def s_gather(k, a, b):
+        s.activation(T.yt[:, 16 * a:16 * b], W.indirect(T.off[:, a:b]), F.Copy).then_inc(S["gy%d" % k], 1)
+
+    for t in v_chunks[:2]:
+        v_right(t, HALF, 257, S["rb%d" % t])
+    counts_to_offsets(0)
+    for t in v_chunks[2:]:
+        v_right(t, HALF, 257, S["rb%d" % t])
+    s.wait_ge(S.set, nset)
+    for q in range(4):
+        b = 64 * q
+        v.wait_ge(S["of%d" % q], 1)
+        s.wait_ge(S["of%d" % q], 1)
         if q == 0:
             for eng in (v, s):
                 eng.wait_ge(S.ldx, 16)
                 eng.wait_ge(S.xarr, nful * len(x_from))
-        for (va, vb), (sa, sb) in zip(v_pieces[q], s_pieces[q]):
-            v.tensor_copy(T.yt[:, 16 * va:16 * vb], W.indirect(T.off[:, va:vb])).then_inc(S["gv%d" % kv], 1)
-            s.activation(T.yt[:, 16 * sa:16 * sb], W.indirect(T.off[:, sa:sb]), F.Copy).then_inc(S["gs%d" % ks], 1)
-            sy.wait_ge(S["gv%d" % kv], 1)
-            sy.dma_start(T.y[:, 16 * va:16 * vb], T.yt[:, 16 * va:16 * vb]).then_inc(S.st, 16)
-            sy.wait_ge(S["gs%d" % ks], 1)
-            sy.dma_start(T.y[:, 16 * sa:16 * sb], T.yt[:, 16 * sa:16 * sb]).then_inc(S.st, 16)
-            kv += 1
-            ks += 1
-            sts += 2
-    sy.wait_ge(S.st, 16 * sts)
+        if q in (0, 3):
+            k = 0 if q == 0 else 4
+            v_gather(k, b, b + 16)
+            s_gather(k, b + 16, b + 32)
+            if q == 0:
+                v_gather(k + 1, b + 32, b + 40)
+                counts_to_offsets(1)
+                v_gather(k + 1, b + 40, b + 46)
+            else:
+                v_gather(k + 1, b + 32, b + 46)
+            s_gather(k + 1, b + 46, b + 64)
+            stores = [(k, b, b + 32, 2), (k + 1, b + 32, b + 64, 3 if q == 0 else 2)]
+        else:
+            k = q + 1
+            v_gather(k, b, b + 22)
+            counts_to_offsets(q + 1)
+            v_gather(k, b + 22, b + 30)
+            s_gather(k, b + 30, b + 64)
+            stores = [(k, b, b + 64, 3)]
+        for k, lo_c, hi_c, n in stores:
+            sy.wait_ge(S["gy%d" % k], n)
+            sy.dma_start(T.y[:, 16 * lo_c:16 * hi_c], T.yt[:, 16 * lo_c:16 * hi_c]).then_inc(S.st, 16)
+    sy.wait_ge(S.st, 16 * 6)

from concourse.bass import DstId, RemoteDMATransfer
from concourse.mybir import AluOpType, ActivationFunctionType

N, J, Q = 6, 256, 4096
MAGIC = 201326592.0

SCRATCH = {
    "lnd": ("dram", [N * 128, 2], "int32"),
    "lni": ("sbuf", [128, 16 * N], "int32"),
    "lnf": ("sbuf", [128, 16 * N], "float32"),
    "pref": ("sbuf", [128, 16 * N + 4], "float32"),
    "ones": ("sbuf", [128, 128], "float32"),
    "tri": ("sbuf", [128, 128], "float32"),
    "qi": ("sbuf", [128, 1], "int32"),
    "qa": ("sbuf", [128, 1], "int32"),
    "qb": ("sbuf", [128, 1], "int32"),
    "qc": ("sbuf", [128, 1], "int32"),
    "qd": ("sbuf", [128, 1], "int32"),
    "off6": ("sbuf", [128, 2], "uint16"),
    "eh": ("sbuf", [128, 96], "float32"),
    "e6": ("sbuf", [128, 16], "float32"),
    "iop": ("sbuf", [128, 128], "bfloat16"),
    "i16": ("sbuf", [128, 264], "bfloat16"),
    "ios": ("sbuf", [128, 264], "float32"),
    "la": ("sbuf", [128, 6 * 128], "bfloat16"),
    "lb": ("sbuf", [128, 6 * 128], "bfloat16"),
    "rr": ("sbuf", [128, 6 * 264], "bfloat16"),
    "off": ("sbuf", [128, 256], "uint16"),
    "win": ("sbuf", [128, 776], "bfloat16"),
    "yt": ("sbuf", [128, Q], "bfloat16"),
    "pe": ("psum", [128, 512], "float32"),
    "p0": ("psum", [128, 512], "float32"),
    "p1": ("psum", [128, 512], "float32"),
    "p2": ("psum", [128, 512], "float32"),
    "p3": ("psum", [128, 512], "float32"),
}
SEMAPHORES = (["ldl", "ldx", "lnin", "lnarr", "xarr", "lsl", "lsx", "one", "tri", "qi", "qs", "i16", "ios", "set", "conv",
               "scan", "e48", "eh", "e6", "st"]
              + ["ch%d" % t for t in range(6)] + ["rb%d" % t for t in range(6)] + ["pq%d" % q for q in range(4)]
              + ["of%d" % q for q in range(4)] + ["gy%d" % k for k in range(6)])


def bits_of(m):
    return [b for b in range(16) if m >> b & 1]


def rank_program(g, core, T, topo):
    r = T.rank_of(core)
    if r is None:
        return
    S = T.sem
    A = AluOpType
    F = ActivationFunctionType
    v, s, pe, sy = g.vector, g.scalar, g.tensor, g.sync
    near = [i for i in (r - 1, r, r + 1) if 0 <= i < N]
    nn = len(near)
    nc = 2 * nn
    nf = near[0]
    ncol = 16 * (near[-1] + 1)
    c0 = 16 * near[0]
    w16 = 16 * nn
    lo = 256 * (near[0] - (r - 1))
    tail = 1 if r >= N - 2 else 0
    whi = lo + 256 * nn + tail
    s_chunks = [t for t in range(nc) if t % 2 == 1]
    v_chunks = [t for t in range(nc) if t % 2 == 0]

    def dest(i):
        rid, pid, _ = topo.addr(T.cores[i])
        return DstId(rid=rid, pnc=pid)

    def is_mate(i):
        return topo.mates(topo.chip(core), topo.chip(T.cores[i]))

    sy.dma_start(T.lnd[128 * r:128 * r + 128, :], T.ln[:]).then_inc(S.ldl, 16)
    s.dma_start(T.win[:, 256:512], T.x[:]).then_inc(S.ldx, 16)
    s.dma_start(T.lni[0:16, 16 * r:16 * r + 16], T.ln[:]).then_inc(S.lnin, 16)

    g.iota(T.qi[:], [[0, 1]], 0, 1).then_inc(S.qi, 1)
    g.wait_ge(S.one, 1)
    g.affine_select(T.tri[0:16, :], T.ones[0:16, :], [[0, 8], [1, 16]], A.is_ge, 0.0, 0, -1).then_inc(S.tri, 1)

    ln_to = sorted([i for i in range(N) if i > r or i == r - 1], key=lambda i: (i in (0, N - 1), is_mate(i)))
    x_to = sorted([i for i in near if i != r], key=is_mate)
    full = topo.mask(core, T.cores[ln_to[0]])
    for i in ln_to:
        full &= topo.mask(core, T.cores[i])
    ebits = bits_of(full)
    few = [b for b in ebits if b % 4 == 0]
    nfew = len(few)
    nful = len(ebits)
    fmask = sum(1 << b for b in few)
    g.wait_ge(S.ldl, 16)
    src = T.lnd[128 * r:128 * r + 128, :]
    g.remote_dma_fused([RemoteDMATransfer(dst_ids=[dest(i) for i in ln_to], dma_engine_mask=fmask, remote_sem=S.lnarr,
                                          srcs=[src], dsts=[src for i in ln_to])], local_sem=S.lsl)
    g.wait_ge(S.ldx, 16)
    g.remote_dma_fused([RemoteDMATransfer(dst_ids=[dest(i) for i in x_to], dma_engine_mask=full, remote_sem=S.xarr,
                                          srcs=[T.win[:, 256:512]],
                                          dsts=[T.win[:, 256 * (r - i + 1):256 * (r - i + 1) + 256] for i in x_to])],
                       local_sem=S.lsx)
    g.wait_ge(S.lsl, nfew)
    g.wait_ge(S.lsx, nful)

    ln_from = [i for i in range(N) if i != r and (i < r or i == r + 1)]
    x_from = [i for i in near if i != r]
    nld = 1

    def load_list(queue, i):
        queue.dma_start(T.lni[0:16, 16 * i:16 * i + 16], T.lnd[128 * i:128 * i + 128, :]).then_inc(S.lnin, 16)

    sy.wait_ge(S.lnarr, nfew * len(ln_from))
    if nf:
        sy.dma_start(T.lni[0:16, 0:16 * nf], T.lnd[0:128 * nf, :]).then_inc(S.lnin, 16)
        nld += 1
    if r + 1 < N:
        load_list(sy, r + 1)
        nld += 1
    if r > 0:
        s.wait_ge(S.lnarr, nfew * len(ln_from))
        load_list(s, r - 1)
        nld += 1

    start = (-float(Q) * r - 7.5) / 16.0
    v.memset(T.ones[0:16, :], 1.0).then_inc(S.one, 1)
    nset = 1
    v.memset(T.pref[0:16, 0:1], start).then_inc(S.set, 1)
    v.memset(T.i16[:, 0:1], -16.0).then_inc(S.i16, 1)
    for p in range(16):
        v.memset(T.iop[:, p:128:16], p - 7.5).then_inc(S.set, 1)
        nset += 1
    if tail:
        v.memset(T.win[:, lo + 256 * nn:lo + 256 * nn + 8], 0.0).then_inc(S.set, 1)
        nset += 1
    v.wait_ge(S.qi, 1)
    v.tensor_scalar(T.qa[:], T.qi[:], 15, None, A.bitwise_and).then_inc(S.qs, 1)
    v.tensor_scalar(T.qb[:], T.qi[:], 4, None, A.logical_shift_right).then_inc(S.qs, 1)
    v.wait_ge(S.qs, 2)
    v.tensor_scalar(T.qc[:], T.qa[:], 8.0, None, A.mult).then_inc(S.qs, 1)
    v.wait_ge(S.qs, 3)
    v.tensor_tensor(T.qd[:], T.qc[:], T.qb[:], A.add).then_inc(S.qs, 1)
    v.wait_ge(S.qs, 4)
    v.tensor_scalar(T.off6[:, 0:1], T.qd[:], float(2 * w16 - 1), None, A.min).then_inc(S.qs, 1)
    have, ni = 1, 1
    while have < 257:
        n = min(have, 257 - have)
        v.wait_ge(S.i16, ni)
        v.tensor_scalar(T.i16[:, have:have + n], T.i16[:, 0:n], 16.0 * have, None, A.add).then_inc(S.i16, 1)
        have += n
        ni += 1
    v.wait_ge(S.i16, ni)
    v.tensor_scalar(T.ios[:, 0:257], T.i16[:, 0:257], -1.0, -8.0, A.mult, A.add).then_inc(S.ios, 1)

    v.wait_ge(S.lnin, 16 * nld)
    v.tensor_copy(T.lnf[0:16, 0:ncol], T.lni[0:16, 0:ncol]).then_inc(S.conv, 1)
    v.wait_ge(S.one, 1)
    v.wait_ge(S.conv, 1)
    v.tensor_tensor_scan(T.pref[0:16, 1:ncol + 1], T.ones[0:16, 0:ncol], T.lnf[0:16, 0:ncol], start,
                         A.mult, A.add).then_inc(S.scan, 1)
    pe.wait_ge(S.tri, 1)
    pe.wait_ge(S.one, 1)
    pe.wait_ge(S.set, nset)
    pe.wait_ge(S.conv, 1)
    pe.matmul(T.pe[:, 0:w16], T.tri[0:16, :], T.lnf[0:16, c0:c0 + w16], True, False)
    pe.wait_ge(S.scan, 1)
    pe.matmul(T.pe[:, 0:w16], T.ones[0:16, :], T.pref[0:16, c0:c0 + w16], False, True).then_inc(S.e48, 1)
    v.wait_ge(S.e48, 1)
    v.tensor_copy(T.eh[:, 0:w16], T.pe[:, 0:w16]).then_inc(S.eh, 1)
    v.tensor_scalar(T.eh[:, w16:2 * w16], T.pe[:, 0:w16], MAGIC, MAGIC, A.add, A.subtract).then_inc(S.eh, 1)
    v.wait_ge(S.qs, 5)
    v.wait_ge(S.eh, 2)
    v.tensor_copy(T.e6[:], T.eh[:, 0:2 * w16].indirect(T.off6[:, 0:1])).then_inc(S.e6, 1)

    HALF = 129

    def v_right(t, a, b, sem):
        v.tensor_scalar(T.rr[:, 264 * t + a:264 * t + b], T.i16[:, a:b], T.e6[:, nc + t:nc + t + 1], -2.0,
                        A.is_ge, A.mult).then_inc(sem, 1)

    v.wait_ge(S.set, nset)
    v.wait_ge(S.e6, 1)
    s.wait_ge(S.ios, 1)
    s.wait_ge(S.e6, 1)
    for t in range(nc):
        ch = S["ch%d" % t]
        e = T.e6[:, t:t + 1]
        h = T.e6[:, nc + t:nc + t + 1]
        v.tensor_scalar(T.la[:, 128 * t:128 * t + 128], T.iop[:], h, e, A.add, A.is_ge).then_inc(ch, 1)
        v.tensor_scalar(T.lb[:, 128 * t:128 * t + 128], T.iop[:], h, e, A.add, A.is_lt).then_inc(ch, 1)
        if t in s_chunks:
            s.activation(T.rr[:, 264 * t:264 * t + 257], T.ios[:, 0:257], F.Sign, bias=h, scale=1.0).then_inc(ch, 1)
        else:
            v_right(t, 0, HALF, ch)

    for q in range(4):
        for t in range(nc):
            if q == 0:
                pe.wait_ge(S["ch%d" % t], 3)
            if q == 2 and t in v_chunks:
                pe.wait_ge(S["rb%d" % t], 1)
            out = T["p%d" % q][:, 0:64]
            b = 264 * t + 64 * q
            pe.matmul(out, T.la[:, 128 * t:128 * t + 128], T.rr[:, b + 1:b + 65], t == 0, False)
            m = pe.matmul(out, T.lb[:, 128 * t:128 * t + 128], T.rr[:, b:b + 64], False, t == nc - 1)
            if t == nc - 1:
                m.then_inc(S["pq%d" % q], 1)

    W = T.win[:, lo:whi]

    def counts_to_offsets(q):
        v.wait_ge(S["pq%d" % q], 1)
        v.tensor_scalar(T.off[:, 64 * q:64 * q + 64], T["p%d" % q][:, 0:64], -128.0 * len(s_chunks), -0.5,
                        A.add, A.mult).then_inc(S["of%d" % q], 1)

    def v_gather(k, a, b):
        v.tensor_copy(T.yt[:, 16 * a:16 * b], W.indirect(T.off[:, a:b])).then_inc(S["gy%d" % k], 1)

    def s_gather(k, a, b):
        s.activation(T.yt[:, 16 * a:16 * b], W.indirect(T.off[:, a:b]), F.Copy).then_inc(S["gy%d" % k], 1)

    for t in v_chunks[:2]:
        v_right(t, HALF, 257, S["rb%d" % t])
    counts_to_offsets(0)
    for t in v_chunks[2:]:
        v_right(t, HALF, 257, S["rb%d" % t])
    s.wait_ge(S.set, nset)
    for q in range(4):
        b = 64 * q
        v.wait_ge(S["of%d" % q], 1)
        s.wait_ge(S["of%d" % q], 1)
        if q == 0:
            for eng in (v, s):
                eng.wait_ge(S.ldx, 16)
                eng.wait_ge(S.xarr, nful * len(x_from))
        if q in (0, 3):
            k = 0 if q == 0 else 4
            v_gather(k, b, b + 16)
            s_gather(k, b + 16, b + 32)
            if q == 0:
                v_gather(k + 1, b + 32, b + 40)
                counts_to_offsets(1)
                v_gather(k + 1, b + 40, b + 46)
            else:
                v_gather(k + 1, b + 32, b + 46)
            s_gather(k + 1, b + 46, b + 64)
            stores = [(k, b, b + 32, 2), (k + 1, b + 32, b + 64, 3 if q == 0 else 2)]
        else:
            k = q + 1
            v_gather(k, b, b + 22)
            counts_to_offsets(q + 1)
            v_gather(k, b + 22, b + 30)
            s_gather(k, b + 30, b + 64)
            stores = [(k, b, b + 64, 3)]
        for k, lo_c, hi_c, n in stores:
            sy.wait_ge(S["gy%d" % k], n)
            sy.dma_start(T.y[:, 16 * lo_c:16 * hi_c], T.yt[:, 16 * lo_c:16 * hi_c]).then_inc(S.st, 16)
    sy.wait_ge(S.st, 16 * 6)
